import numpy as np
import ml_dtypes


def mxq(x, axis, fmt="e4m3"):
    dtype, down = {"e4m3": (ml_dtypes.float8_e4m3fn, 7), "e5m2": (ml_dtypes.float8_e5m2, 14)}[fmt]
    v = np.moveaxis(np.asarray(x, np.float32).astype(ml_dtypes.bfloat16).astype(np.float64), axis, -1)
    blocks = v.reshape(v.shape[:-1] + (-1, 32))
    amax = np.abs(blocks).max(-1, keepdims=True)
    byte = np.maximum(np.where(amax > 0, np.frexp(amax)[1] - 1 + 127, 0) - down, 1)
    scale = np.exp2(byte - 127.0)
    codes = (blocks / scale).astype(np.float32).astype(dtype).astype(np.float64)
    return np.moveaxis((codes * scale).reshape(v.shape), -1, axis)


WIDE = False


def mx_kscale(k):
    if not WIDE:
        return np.ones(k)
    levels = np.array([10, -10, 5, -5, 0])
    if k % 512:
        return np.exp2(np.random.permutation(np.resize(levels, k // 32))).repeat(32)
    a = np.empty((k // 512, 16))
    for p in range(k // 512):
        a[p, :8] = np.random.permutation(np.resize(levels, 8))
        for g in range(8):
            far = levels[np.abs(levels - a[p, g]) >= 10]
            a[p, g + 8] = far[np.random.randint(len(far))]
    return np.exp2(a.ravel()).repeat(32)


def f64(x):
    return np.asarray(x).astype(np.float64)


def striped(idx):
    return np.tile(np.asarray(idx).reshape(-1, 16).T, (8, 1)).astype(np.uint16)


def unstriped(offs):
    return offs[:16].T.reshape(-1).astype(np.int64)


E2M1 = np.array([0.0, 0.5, 1.0, 1.5, 2.0, 3.0, 4.0, 6.0, -0.0, -0.5, -1.0, -1.5, -2.0, -3.0, -4.0, -6.0])


def pack_weight(w, fmt):
    k, n = w.shape
    w = f64(np.asarray(w, np.float32).astype(ml_dtypes.bfloat16)).reshape(k // 32, 32, n)
    amax = np.abs(w).max(1)
    if fmt == "e4m3":
        byte = np.frexp(amax)[1] - 1 + 127 - 7
    else:
        mant, ex = np.frexp(amax / 6.0)
        byte = np.where(mant > 0.5, ex, ex - 1) + 127
    byte = np.clip(np.where(amax > 0, byte, 1), 1, 254)
    scaled = (w * np.exp2(127.0 - byte)[:, None, :]).reshape(k, n).astype(np.float32)
    by_word = np.ascontiguousarray(scaled.reshape(k // 512, 128, 4, n).transpose(0, 1, 3, 2))
    if fmt == "e4m3":
        words = by_word.astype(ml_dtypes.float8_e4m3fn).view(np.uint8)
    else:
        c = by_word.astype(ml_dtypes.float4_e2m1fn).view(np.uint8) & 0xF
        words = (c[..., 0::2] | (c[..., 1::2] << 4)).reshape(k // 512, 128, 2 * n)
    return np.ascontiguousarray(words), np.ascontiguousarray(byte.astype(np.uint8).reshape(k // 512, 16, n))


def unpack_weight(words, scales, fmt):
    g, _, n = scales.shape
    words = np.ascontiguousarray(words).reshape(g, 128, n, -1)
    if fmt == "e4m3":
        vals = words.view(ml_dtypes.float8_e4m3fn).astype(np.float64)
    else:
        nib = np.empty((g, 128, n, 4), np.uint8)
        nib[..., 0::2] = words & 0xF
        nib[..., 1::2] = words >> 4
        vals = E2M1[nib]
    vals = vals * np.repeat(np.exp2(scales.astype(np.float64) - 127.0), 8, axis=1)[..., None]
    return vals.transpose(0, 1, 3, 2).reshape(g * 512, n)


K, L, J, I, T, N = 2048, 2048, 512, 512, 512, 512


def setup_inputs():
    n = np.random.standard_normal
    idx = np.random.permutation(K)[:J]
    idx2 = np.random.permutation(L)[:I]
    fk = mx_kscale(K)
    fj = mx_kscale(J)
    fi = mx_kscale(I)
    tj = np.ones(K)
    tj[idx] = fj
    ti = np.ones(L)
    ti[idx2] = fi
    xbp = pack_weight(n((K, T)) / fk[:, None], "e2m1")
    wbp = pack_weight(n((K, N)) * 1 / np.sqrt(K) * fk[:, None], "e4m3")
    wop = pack_weight(n((J, N)) * 1 / np.sqrt(J) * fj[:, None], "e2m1")
    vop = pack_weight(n((I, N)) * 1 / np.sqrt(I) * fi[:, None], "e4m3")
    return {
        "xb_words": xbp[0],
        "xb_scales": xbp[1],
        "wb_words": wbp[0],
        "wb_scales": wbp[1],
        "xt": (n((T, K)) / tj).astype(np.float32),
        "wo_words": wop[0],
        "wo_scales": wop[1],
        "zt": (n((T, L)) / ti).astype(np.float32),
        "vo_words": vop[0],
        "vo_scales": vop[1],
        "b": (np.random.uniform(-0.5, 0.5, (N, 1))).astype(np.float32),
        "offs": striped(idx),
        "offs2": striped(idx2),
    }


def reference(xb_words, xb_scales, wb_words, wb_scales, xt, wo_words, wo_scales, zt, vo_words, vo_scales, b, offs, offs2):
    idx = unstriped(offs)
    idx2 = unstriped(offs2)
    xbu = unpack_weight(xb_words, xb_scales, "e2m1")
    wbu = unpack_weight(wb_words, wb_scales, "e4m3")
    wou = unpack_weight(wo_words, wo_scales, "e2m1")
    vou = unpack_weight(vo_words, vo_scales, "e4m3")
    xo = f64(xt)[:, idx].T
    zo = f64(zt)[:, idx2].T
    xoq = mxq(xo, 0, "e4m3")
    zoq = mxq(zo, 0, "e4m3")
    z = wbu.T @ xbu + wou.T @ xoq + vou.T @ zoq
    y = z + f64(b)
    return y

@@ -1,0 +1,158 @@
+from contextlib import ExitStack
+
+import concourse.mybir as mybir
+from concourse.masks import make_identity
+
+K, J, T, N = 2048, 512, 512, 512
+FLOPS = 2 * (K + 2 * J) * N * T
+
+F32 = mybir.dt.float32
+BF16 = mybir.dt.bfloat16
+I32 = mybir.dt.int32
+U32 = mybir.dt.uint32
+U16 = mybir.dt.uint16
+U8 = mybir.dt.uint8
+FP8X4 = mybir.dt.float8_e4m3fn_x4
+FP4X4 = mybir.dt.float4_e2m1fn_x4
+ACT = mybir.ActivationFunctionType
+
+P = 128
+PASSES = K // 512
+CHUNKS = T // P
+N_TILES = N // P
+VO_ROW = 4
+SPANS = ((0, 2), (2, 1), (3, 1))
+
+
+def load_scale_rows(queue, plane, scales, first, which):
+    rows = scales.bitcast(I32).rearrange("z (q r) c -> r q z c", r=4)
+    for r in which:
+        queue.dma_start(out=plane[first + r:P:32].bitcast(I32), in_=rows[r])
+
+
+def tile_list_outlier_streams_kernel(tc, xb_words, xb_scales, wb_words, wb_scales, xt, wo_words, wo_scales,
+                                        zt, vo_words, vo_scales, b, offs, offs2, out):
+    nc = tc.nc
+    with ExitStack() as ctx:
+        keep = ctx.enter_context(tc.tile_pool(name="keep", bufs=1))
+        work = ctx.enter_context(tc.tile_pool(name="work", bufs=2))
+        sums = ctx.enter_context(tc.psum_pool(name="sums", bufs=1))
+        turn = ctx.enter_context(tc.psum_pool(name="turn", bufs=2))
+
+        x_list = keep.tile([P, J // 16], U16, name="x_list")
+        z_list = keep.tile([P, J // 16], U16, name="z_list")
+        x_rows = [keep.tile([P, K], F32, name="x_rows%d" % c) for c in range(CHUNKS)]
+        z_rows = [keep.tile([P, K], F32, name="z_rows%d" % c) for c in range(CHUNKS)]
+        xb_codes = keep.tile([P, PASSES, 2 * T], U8, name="xb_codes", align_bytes=64)
+        wb_codes = keep.tile([P, PASSES, 4 * N], U8, name="wb_codes", align_bytes=64)
+        wo_codes = keep.tile([P, 2 * N], U8, name="wo_codes", align_bytes=64)
+        vo_codes = keep.tile([P, 4 * N], U8, name="vo_codes", align_bytes=64)
+        xb_plane = keep.tile([P, PASSES, T], U8, name="xb_plane", align_bytes=64)
+        wb_plane = keep.tile([P, PASSES, N], U8, name="wb_plane", align_bytes=64)
+        wo_plane = keep.tile([P, 1, N], U8, name="wo_plane", align_bytes=64)
+        vo_plane = keep.tile([P, 1, N], U8, name="vo_plane", align_bytes=64)
+        ident = keep.tile([P, P], F32, name="ident")
+        bias_rows = keep.tile([P, P], F32, name="bias_rows")
+        bias = keep.tile([P, N_TILES], F32, name="bias")
+
+        def load_rows(tiles, src, c):
+            nc.sync.dma_start(out=tiles[c][:], in_=src[c * P:(c + 1) * P, :])
+
+        make_identity(nc, ident[:])
+        nc.vector.memset(bias_rows[:], 0.0)
+
+        load_scale_rows(nc.gpsimd, wb_plane, wb_scales, 0, range(4))
+        nc.gpsimd.dma_start(out=bias_rows[0:N_TILES, :], in_=b.rearrange("(c p) o -> c (p o)", p=P))
+
+        nc.sync.dma_start(out=wb_codes[:].bitcast(I32),
+                          in_=wb_words.rearrange("z p n r -> p z (n r)").bitcast(I32))
+        load_scale_rows(nc.sync, xb_plane, xb_scales, 0, (0, 1))
+        nc.sync.dma_start(out=xb_codes[:].bitcast(I32), in_=xb_words.rearrange("z p c -> p z c").bitcast(I32))
+        load_scale_rows(nc.sync, xb_plane, xb_scales, 0, (2, 3))
+        load_rows(x_rows, xt, 0)
+        nc.sync.dma_start(x_list[:], offs)
+        load_rows(x_rows, xt, 1)
+        nc.sync.dma_start(out=wo_codes[:].bitcast(I32), in_=wo_words[0].bitcast(I32))
+        load_scale_rows(nc.sync, wo_plane, wo_scales, 0, (0, 1))
+        load_rows(x_rows, xt, 2)
+        load_scale_rows(nc.sync, wo_plane, wo_scales, 0, (2, 3))
+        load_rows(x_rows, xt, 3)
+        nc.sync.dma_start(z_list[:], offs2)
+        nc.sync.dma_start(out=vo_codes[:].bitcast(I32),
+                          in_=vo_words[0].rearrange("p n r -> p (n r)").bitcast(I32))
+        load_scale_rows(nc.sync, vo_plane, vo_scales, VO_ROW, (0, 1))
+        load_rows(z_rows, zt, 0)
+        load_scale_rows(nc.sync, vo_plane, vo_scales, VO_ROW, (2, 3))
+        for c in range(1, CHUNKS):
+            load_rows(z_rows, zt, c)
+
+        def quantise_listed(rows, offsets, name):
+            picked = work.tile([P, J], BF16, name="picked", align_bytes=64)
+            half = J // 2
+            nc.vector.tensor_copy(picked[:, 0:half], rows[:].indirect(offsets[:, 0:half // 16]))
+            nc.scalar.activation(picked[:, half:J], rows[:].indirect(offsets[:, half // 16:J // 16]), ACT.Copy)
+            pairs = picked[:].bitcast(F32)
+            turned = turn.tile([P, 2, P], F32, name="turned")
+            for u in range(2):
+                nc.tensor.transpose(turned[:, u, :], pairs[:, u:J // 2:2], ident[:])
+            grouped = work.tile([P, J], BF16, name="grouped", align_bytes=64)
+            nc.scalar.copy(out=grouped[:].bitcast(F32).rearrange("p (t u) -> p t u", u=2),
+                           in_=turned[:].rearrange("p u t -> p t u"))
+            codes = keep.tile([P, P], U32, name=name + "_codes", align_bytes=64)
+            plane = keep.tile([P, P], U8, name=name + "_plane", align_bytes=64)
+            nc.vector.quantize_mx(out=codes[:].bitcast(FP8X4), scales=plane[:], in_=grouped[:])
+            return codes, plane
+
+        banks = [[sums.tile([P, 2, count * P], F32, name="bank%d_%d" % (first, h)) for h in range(2)]
+                 for first, count in SPANS]
+
+        def add_listed(s, c, quantised, weight_tile, weight_plane, opens, closes):
+            first = SPANS[s][0]
+            codes, plane = quantised
+            for nt in range(N_TILES):
+                nc.tensor.matmul_mx(
+                    out=banks[s][nt // 2][:, nt % 2, (c - first) * P:(c - first + 1) * P],
+                    lhsT=weight_tile(nt), lhsT_scale=weight_plane[:, 0, nt * P:(nt + 1) * P],
+                    rhs=codes[:].bitcast(FP8X4), rhs_scale=plane[:],
+                    start=opens and nt % 2 == 0, stop=closes and nt % 2 == 1)
+
+        def wo_tile(nt):
+            return wo_codes[:, 2 * nt * P:2 * (nt + 1) * P].bitcast(FP4X4)
+
+        def vo_tile(nt):
+            return vo_codes[:, 4 * nt * P:4 * (nt + 1) * P].bitcast(FP8X4)
+
+        for s, (first, count) in enumerate(SPANS):
+            t0, t1 = first * P, (first + count) * P
+            for nt in range(N_TILES):
+                for z in range(PASSES):
+                    nc.tensor.matmul_mx(
+                        out=banks[s][nt // 2][:, nt % 2, :],
+                        lhsT=wb_codes[:, z, 4 * nt * P:4 * (nt + 1) * P].bitcast(FP8X4),
+                        lhsT_scale=wb_plane[:, z, nt * P:(nt + 1) * P],
+                        rhs=xb_codes[:, z, 2 * t0:2 * t1].bitcast(FP4X4), rhs_scale=xb_plane[:, z, t0:t1],
+                        start=z == 0 and nt % 2 == 0, stop=False)
+
+        for s, (first, count) in enumerate(SPANS):
+            for c in range(first, first + count):
+                add_listed(s, c, quantise_listed(x_rows[c], x_list, "xq%d" % c), wo_tile, wo_plane[:],
+                           False, False)
+
+        bias_turned = turn.tile([P, 2, P], F32, name="turned")
+        nc.tensor.transpose(bias_turned[:, 0, :], bias_rows[:], ident[:])
+        nc.vector.tensor_copy(bias[:], bias_turned[:, 0, 0:N_TILES])
+
+        out_tiles = out.rearrange("(c p) t -> p c t", p=P)
+        for s, (first, count) in enumerate(SPANS):
+            t0, t1 = first * P, (first + count) * P
+            for c in range(first, first + count):
+                add_listed(s, c, quantise_listed(z_rows[c], z_list, "zq%d" % c), vo_tile, vo_plane[VO_ROW:P],
+                           False, c == first + count - 1)
+            low = keep.tile([P, 2, t1 - t0], F32, name="low%d" % s)
+            nc.vector.tensor_tensor(low[:], banks[s][0][:], bias[:, 0:2].unsqueeze(2).to_broadcast([P, 2, t1 - t0]),
+                                    mybir.AluOpType.add)
+            nc.sync.dma_start(out=out_tiles[:, 0:2, t0:t1], in_=low[:])
+            high = keep.tile([P, 2, t1 - t0], F32, name="high%d" % s)
+            for i in range(2):
+                nc.scalar.activation(high[:, i, :], banks[s][1][:, i, :], ACT.Identity, bias=bias[:, 2 + i:3 + i])
+            nc.sync.dma_start(out=out_tiles[:, 2:4, t0:t1], in_=high[:])

@@ -21,13 +21,8 @@ PASSES = K // 512
 CHUNKS = T // P
 N_TILES = N // P
 VO_ROW = 4
+EARLY = 3
 SPANS = ((0, 2), (2, 1), (3, 1))
-
-
-def load_scale_rows(queue, plane, scales, first, which):
-    rows = scales.bitcast(I32).rearrange("z (q r) c -> r q z c", r=4)
-    for r in which:
-        queue.dma_start(out=plane[first + r:P:32].bitcast(I32), in_=rows[r])
 
 
 def tile_list_outlier_streams_kernel(tc, xb_words, xb_scales, wb_words, wb_scales, xt, wo_words, wo_scales,
@@ -35,7 +30,6 @@ def tile_list_outlier_streams_kernel(tc, xb_words, xb_scales, wb_words, wb_scale
     nc = tc.nc
     with ExitStack() as ctx:
         keep = ctx.enter_context(tc.tile_pool(name="keep", bufs=1))
-        work = ctx.enter_context(tc.tile_pool(name="work", bufs=2))
         sums = ctx.enter_context(tc.psum_pool(name="sums", bufs=1))
         turn = ctx.enter_context(tc.psum_pool(name="turn", bufs=2))
 
@@ -43,8 +37,10 @@ def tile_list_outlier_streams_kernel(tc, xb_words, xb_scales, wb_words, wb_scale
         z_list = keep.tile([P, J // 16], U16, name="z_list")
         x_rows = [keep.tile([P, K], F32, name="x_rows%d" % c) for c in range(CHUNKS)]
         z_rows = [keep.tile([P, K], F32, name="z_rows%d" % c) for c in range(CHUNKS)]
-        xb_codes = keep.tile([P, PASSES, 2 * T], U8, name="xb_codes", align_bytes=64)
-        wb_codes = keep.tile([P, PASSES, 4 * N], U8, name="wb_codes", align_bytes=64)
+        xb_early = keep.tile([P, EARLY, 2 * T], U8, name="xb_early", align_bytes=64)
+        wb_early = keep.tile([P, EARLY, 4 * N], U8, name="wb_early", align_bytes=64)
+        xb_late = keep.tile([P, PASSES - EARLY, 2 * T], U8, name="xb_late", align_bytes=64)
+        wb_late = keep.tile([P, PASSES - EARLY, 4 * N], U8, name="wb_late", align_bytes=64)
         wo_codes = keep.tile([P, 2 * N], U8, name="wo_codes", align_bytes=64)
         vo_codes = keep.tile([P, 4 * N], U8, name="vo_codes", align_bytes=64)
         xb_plane = keep.tile([P, PASSES, T], U8, name="xb_plane", align_bytes=64)
@@ -58,96 +54,94 @@ def tile_list_outlier_streams_kernel(tc, xb_words, xb_scales, wb_words, wb_scale
         def load_rows(tiles, src, c):
             nc.sync.dma_start(out=tiles[c][:], in_=src[c * P:(c + 1) * P, :])
 
+        def load_codes(tile, words):
+            nc.sync.dma_start(out=tile[:].bitcast(I32), in_=words.bitcast(I32))
+
+        def load_scale_rows(queue, plane, scales, first, which):
+            rows = scales.bitcast(I32).rearrange("z (q r) c -> r q z c", r=4)
+            for r in which:
+                queue.dma_start(out=plane[first + r:P:32].bitcast(I32), in_=rows[r])
+
         make_identity(nc, ident[:])
         nc.vector.memset(bias_rows[:], 0.0)
 
-        load_scale_rows(nc.gpsimd, wb_plane, wb_scales, 0, range(4))
-        nc.gpsimd.dma_start(out=bias_rows[0:N_TILES, :], in_=b.rearrange("(c p) o -> c (p o)", p=P))
-
-        nc.sync.dma_start(out=wb_codes[:].bitcast(I32),
-                          in_=wb_words.rearrange("z p n r -> p z (n r)").bitcast(I32))
-        load_scale_rows(nc.sync, xb_plane, xb_scales, 0, (0, 1))
-        nc.sync.dma_start(out=xb_codes[:].bitcast(I32), in_=xb_words.rearrange("z p c -> p z c").bitcast(I32))
-        load_scale_rows(nc.sync, xb_plane, xb_scales, 0, (2, 3))
         load_rows(x_rows, xt, 0)
         nc.sync.dma_start(x_list[:], offs)
+        load_scale_rows(nc.sync, wb_plane, wb_scales, 0, (0, 1, 2, 3,))
+        nc.sync.dma_start(out=bias_rows[0:N_TILES, :], in_=b.rearrange("(c p) o -> c (p o)", p=P))
         load_rows(x_rows, xt, 1)
-        nc.sync.dma_start(out=wo_codes[:].bitcast(I32), in_=wo_words[0].bitcast(I32))
-        load_scale_rows(nc.sync, wo_plane, wo_scales, 0, (0, 1))
-        load_rows(x_rows, xt, 2)
-        load_scale_rows(nc.sync, wo_plane, wo_scales, 0, (2, 3))
-        load_rows(x_rows, xt, 3)
+        load_scale_rows(nc.sync, xb_plane, xb_scales, 0, (0, 1, 2, 3,))
+        load_codes(xb_early, xb_words[0:EARLY].rearrange("z p c -> p z c"))
+        load_codes(wo_codes, wo_words[0])
+        load_codes(wb_early, wb_words[0:EARLY].rearrange("z p n r -> p z (n r)"))
+        load_scale_rows(nc.sync, wo_plane, wo_scales, 0, (0, 1, 2, 3,))
         nc.sync.dma_start(z_list[:], offs2)
-        nc.sync.dma_start(out=vo_codes[:].bitcast(I32),
-                          in_=vo_words[0].rearrange("p n r -> p (n r)").bitcast(I32))
-        load_scale_rows(nc.sync, vo_plane, vo_scales, VO_ROW, (0, 1))
+        load_codes(vo_codes, vo_words[0].rearrange("p n r -> p (n r)"))
         load_rows(z_rows, zt, 0)
-        load_scale_rows(nc.sync, vo_plane, vo_scales, VO_ROW, (2, 3))
-        for c in range(1, CHUNKS):
-            load_rows(z_rows, zt, c)
+        load_scale_rows(nc.sync, vo_plane, vo_scales, VO_ROW, (0, 1, 2, 3,))
+        load_rows(z_rows, zt, 1)
+        load_rows(x_rows, xt, 2)
+        load_rows(z_rows, zt, 2)
+        load_rows(x_rows, xt, 3)
+        load_codes(wb_late, wb_words[EARLY:PASSES].rearrange("z p n r -> p z (n r)"))
+        load_codes(xb_late, xb_words[EARLY:PASSES].rearrange("z p c -> p z c"))
+        load_rows(z_rows, zt, 3)
 
-        def quantise_listed(rows, offsets, name):
-            picked = work.tile([P, J], BF16, name="picked", align_bytes=64)
-            half = J // 2
-            nc.vector.tensor_copy(picked[:, 0:half], rows[:].indirect(offsets[:, 0:half // 16]))
-            nc.scalar.activation(picked[:, half:J], rows[:].indirect(offsets[:, half // 16:J // 16]), ACT.Copy)
-            pairs = picked[:].bitcast(F32)
-            turned = turn.tile([P, 2, P], F32, name="turned")
-            for u in range(2):
-                nc.tensor.transpose(turned[:, u, :], pairs[:, u:J // 2:2], ident[:])
-            grouped = work.tile([P, J], BF16, name="grouped", align_bytes=64)
-            nc.scalar.copy(out=grouped[:].bitcast(F32).rearrange("p (t u) -> p t u", u=2),
-                           in_=turned[:].rearrange("p u t -> p t u"))
-            codes = keep.tile([P, P], U32, name=name + "_codes", align_bytes=64)
-            plane = keep.tile([P, P], U8, name=name + "_plane", align_bytes=64)
+        def quantise_listed(sources, name):
+            count = len(sources)
+            turned = turn.tile([P, count, 2, P], F32, name="turned")
+            for i, (rows, offsets) in enumerate(sources):
+                picked = keep.tile([P, J], BF16, name="%s_picked%d" % (name, i), align_bytes=64)
+                half = J // 2
+                nc.vector.tensor_copy(picked[:, 0:half], rows[:].indirect(offsets[:, 0:half // 16]))
+                nc.scalar.activation(picked[:, half:J], rows[:].indirect(offsets[:, half // 16:J // 16]), ACT.Copy)
+                pairs = picked[:].bitcast(F32)
+                for u in range(2):
+                    nc.tensor.transpose(turned[:, i, u, :], pairs[:, u:J // 2:2], ident[:])
+            grouped = keep.tile([P, count * J], BF16, name=name + "_grouped", align_bytes=64)
+            nc.scalar.copy(out=grouped[:].bitcast(F32).rearrange("p (i t u) -> p i t u", i=count, u=2),
+                           in_=turned[:].rearrange("p i u t -> p i t u"))
+            codes = keep.tile([P, count * P], U32, name=name + "_codes", align_bytes=64)
+            plane = keep.tile([P, count * P], U8, name=name + "_plane", align_bytes=64)
             nc.vector.quantize_mx(out=codes[:].bitcast(FP8X4), scales=plane[:], in_=grouped[:])
             return codes, plane
 
         banks = [[sums.tile([P, 2, count * P], F32, name="bank%d_%d" % (first, h)) for h in range(2)]
                  for first, count in SPANS]
 
-        def add_listed(s, c, quantised, weight_tile, weight_plane, opens, closes):
-            first = SPANS[s][0]
-            codes, plane = quantised
+        def add_listed(s, codes, plane, weight_tile, weight_plane, closes):
             for nt in range(N_TILES):
                 nc.tensor.matmul_mx(
-                    out=banks[s][nt // 2][:, nt % 2, (c - first) * P:(c - first + 1) * P],
+                    out=banks[s][nt // 2][:, nt % 2, :],
                     lhsT=weight_tile(nt), lhsT_scale=weight_plane[:, 0, nt * P:(nt + 1) * P],
-                    rhs=codes[:].bitcast(FP8X4), rhs_scale=plane[:],
-                    start=opens and nt % 2 == 0, stop=closes and nt % 2 == 1)
+                    rhs=codes.bitcast(FP8X4), rhs_scale=plane,
+                    start=False, stop=closes and nt % 2 == 1)
 
-        def wo_tile(nt):
-            return wo_codes[:, 2 * nt * P:2 * (nt + 1) * P].bitcast(FP4X4)
+        def add_x(s, codes, plane):
+            add_listed(s, codes, plane, lambda nt: wo_codes[:, 2 * nt * P:2 * (nt + 1) * P].bitcast(FP4X4),
+                       wo_plane[:], False)
 
-        def vo_tile(nt):
-            return vo_codes[:, 4 * nt * P:4 * (nt + 1) * P].bitcast(FP8X4)
+        def add_z(s, codes, plane, closes):
+            add_listed(s, codes, plane, lambda nt: vo_codes[:, 4 * nt * P:4 * (nt + 1) * P].bitcast(FP8X4),
+                       vo_plane[VO_ROW:P], closes)
 
-        for s, (first, count) in enumerate(SPANS):
+        def add_base(s, passes, wb_codes, xb_codes, closes):
+            first, count = SPANS[s]
             t0, t1 = first * P, (first + count) * P
             for nt in range(N_TILES):
-                for z in range(PASSES):
+                for i, z in enumerate(passes):
                     nc.tensor.matmul_mx(
                         out=banks[s][nt // 2][:, nt % 2, :],
-                        lhsT=wb_codes[:, z, 4 * nt * P:4 * (nt + 1) * P].bitcast(FP8X4),
+                        lhsT=wb_codes[:, i, 4 * nt * P:4 * (nt + 1) * P].bitcast(FP8X4),
                         lhsT_scale=wb_plane[:, z, nt * P:(nt + 1) * P],
-                        rhs=xb_codes[:, z, 2 * t0:2 * t1].bitcast(FP4X4), rhs_scale=xb_plane[:, z, t0:t1],
-                        start=z == 0 and nt % 2 == 0, stop=False)
-
-        for s, (first, count) in enumerate(SPANS):
-            for c in range(first, first + count):
-                add_listed(s, c, quantise_listed(x_rows[c], x_list, "xq%d" % c), wo_tile, wo_plane[:],
-                           False, False)
-
-        bias_turned = turn.tile([P, 2, P], F32, name="turned")
-        nc.tensor.transpose(bias_turned[:, 0, :], bias_rows[:], ident[:])
-        nc.vector.tensor_copy(bias[:], bias_turned[:, 0, 0:N_TILES])
+                        rhs=xb_codes[:, i, 2 * t0:2 * t1].bitcast(FP4X4), rhs_scale=xb_plane[:, z, t0:t1],
+                        start=z == 0 and nt % 2 == 0, stop=closes and z == PASSES - 1 and nt % 2 == 1)
 
         out_tiles = out.rearrange("(c p) t -> p c t", p=P)
-        for s, (first, count) in enumerate(SPANS):
+
+        def store(s):
+            first, count = SPANS[s]
             t0, t1 = first * P, (first + count) * P
-            for c in range(first, first + count):
-                add_listed(s, c, quantise_listed(z_rows[c], z_list, "zq%d" % c), vo_tile, vo_plane[VO_ROW:P],
-                           False, c == first + count - 1)
             low = keep.tile([P, 2, t1 - t0], F32, name="low%d" % s)
             nc.vector.tensor_tensor(low[:], banks[s][0][:], bias[:, 0:2].unsqueeze(2).to_broadcast([P, 2, t1 - t0]),
                                     mybir.AluOpType.add)
@@ -156,3 +150,26 @@ def tile_list_outlier_streams_kernel(tc, xb_words, xb_scales, wb_words, wb_scale
             for i in range(2):
                 nc.scalar.activation(high[:, i, :], banks[s][1][:, i, :], ACT.Identity, bias=bias[:, 2 + i:3 + i])
             nc.sync.dma_start(out=out_tiles[:, 2:4, t0:t1], in_=high[:])
+
+        bias_turned = turn.tile([P, 1, 2, P], F32, name="turned")
+        nc.tensor.transpose(bias_turned[:, 0, 0, :], bias_rows[:], ident[:])
+        nc.vector.tensor_copy(bias[:], bias_turned[:, 0, 0, 0:N_TILES])
+
+        x_first = quantise_listed([(x_rows[0], x_list), (x_rows[1], x_list)], "xq0")
+        for s in range(len(SPANS)):
+            add_base(s, range(EARLY), wb_early, xb_early, False)
+        add_x(0, x_first[0][:], x_first[1][:])
+        codes, plane = quantise_listed([(z_rows[0], z_list), (z_rows[1], z_list)], "zq0")
+        add_z(0, codes[:], plane[:], False)
+        codes, plane = quantise_listed([(x_rows[2], x_list), (z_rows[2], z_list)], "xz1")
+        add_x(1, codes[:, 0:P], plane[:, 0:P])
+        add_z(1, codes[:, P:2 * P], plane[:, P:2 * P], False)
+        codes, plane = quantise_listed([(x_rows[3], x_list)], "xq2")
+        for s in range(len(SPANS)):
+            add_base(s, range(EARLY, PASSES), wb_late, xb_late, s < 2)
+            if s < 2:
+                store(s)
+        add_x(2, codes[:], plane[:])
+        codes, plane = quantise_listed([(z_rows[3], z_list)], "zq2")
+        add_z(2, codes[:], plane[:], True)
+        store(2)

from contextlib import ExitStack

import concourse.mybir as mybir
from concourse.masks import make_identity

K, J, T, N = 2048, 512, 512, 512
FLOPS = 2 * (K + 2 * J) * N * T

F32 = mybir.dt.float32
BF16 = mybir.dt.bfloat16
I32 = mybir.dt.int32
U32 = mybir.dt.uint32
U16 = mybir.dt.uint16
U8 = mybir.dt.uint8
FP8X4 = mybir.dt.float8_e4m3fn_x4
FP4X4 = mybir.dt.float4_e2m1fn_x4
ACT = mybir.ActivationFunctionType

P = 128
PASSES = K // 512
CHUNKS = T // P
N_TILES = N // P
VO_ROW = 4
EARLY = 3
SPANS = ((0, 2), (2, 1), (3, 1))


def tile_list_outlier_streams_kernel(tc, xb_words, xb_scales, wb_words, wb_scales, xt, wo_words, wo_scales,
                                        zt, vo_words, vo_scales, b, offs, offs2, out):
    nc = tc.nc
    with ExitStack() as ctx:
        keep = ctx.enter_context(tc.tile_pool(name="keep", bufs=1))
        sums = ctx.enter_context(tc.psum_pool(name="sums", bufs=1))
        turn = ctx.enter_context(tc.psum_pool(name="turn", bufs=2))

        x_list = keep.tile([P, J // 16], U16, name="x_list")
        z_list = keep.tile([P, J // 16], U16, name="z_list")
        x_rows = [keep.tile([P, K], F32, name="x_rows%d" % c) for c in range(CHUNKS)]
        z_rows = [keep.tile([P, K], F32, name="z_rows%d" % c) for c in range(CHUNKS)]
        xb_early = keep.tile([P, EARLY, 2 * T], U8, name="xb_early", align_bytes=64)
        wb_early = keep.tile([P, EARLY, 4 * N], U8, name="wb_early", align_bytes=64)
        xb_late = keep.tile([P, PASSES - EARLY, 2 * T], U8, name="xb_late", align_bytes=64)
        wb_late = keep.tile([P, PASSES - EARLY, 4 * N], U8, name="wb_late", align_bytes=64)
        wo_codes = keep.tile([P, 2 * N], U8, name="wo_codes", align_bytes=64)
        vo_codes = keep.tile([P, 4 * N], U8, name="vo_codes", align_bytes=64)
        xb_plane = keep.tile([P, PASSES, T], U8, name="xb_plane", align_bytes=64)
        wb_plane = keep.tile([P, PASSES, N], U8, name="wb_plane", align_bytes=64)
        wo_plane = keep.tile([P, 1, N], U8, name="wo_plane", align_bytes=64)
        vo_plane = keep.tile([P, 1, N], U8, name="vo_plane", align_bytes=64)
        ident = keep.tile([P, P], F32, name="ident")
        bias_rows = keep.tile([P, P], F32, name="bias_rows")
        bias = keep.tile([P, N_TILES], F32, name="bias")

        def load_rows(tiles, src, c):
            nc.sync.dma_start(out=tiles[c][:], in_=src[c * P:(c + 1) * P, :])

        def load_codes(tile, words):
            nc.sync.dma_start(out=tile[:].bitcast(I32), in_=words.bitcast(I32))

        def load_scale_rows(queue, plane, scales, first, which):
            rows = scales.bitcast(I32).rearrange("z (q r) c -> r q z c", r=4)
            for r in which:
                queue.dma_start(out=plane[first + r:P:32].bitcast(I32), in_=rows[r])

        make_identity(nc, ident[:])
        nc.vector.memset(bias_rows[:], 0.0)

        load_rows(x_rows, xt, 0)
        nc.sync.dma_start(x_list[:], offs)
        load_scale_rows(nc.sync, wb_plane, wb_scales, 0, (0, 1, 2, 3,))
        nc.sync.dma_start(out=bias_rows[0:N_TILES, :], in_=b.rearrange("(c p) o -> c (p o)", p=P))
        load_rows(x_rows, xt, 1)
        load_scale_rows(nc.sync, xb_plane, xb_scales, 0, (0, 1, 2, 3,))
        load_codes(xb_early, xb_words[0:EARLY].rearrange("z p c -> p z c"))
        load_codes(wo_codes, wo_words[0])
        load_codes(wb_early, wb_words[0:EARLY].rearrange("z p n r -> p z (n r)"))
        load_scale_rows(nc.sync, wo_plane, wo_scales, 0, (0, 1, 2, 3,))
        nc.sync.dma_start(z_list[:], offs2)
        load_codes(vo_codes, vo_words[0].rearrange("p n r -> p (n r)"))
        load_rows(z_rows, zt, 0)
        load_scale_rows(nc.sync, vo_plane, vo_scales, VO_ROW, (0, 1, 2, 3,))
        load_rows(z_rows, zt, 1)
        load_rows(x_rows, xt, 2)
        load_rows(z_rows, zt, 2)
        load_rows(x_rows, xt, 3)
        load_codes(wb_late, wb_words[EARLY:PASSES].rearrange("z p n r -> p z (n r)"))
        load_codes(xb_late, xb_words[EARLY:PASSES].rearrange("z p c -> p z c"))
        load_rows(z_rows, zt, 3)

        def quantise_listed(sources, name):
            count = len(sources)
            turned = turn.tile([P, count, 2, P], F32, name="turned")
            for i, (rows, offsets) in enumerate(sources):
                picked = keep.tile([P, J], BF16, name="%s_picked%d" % (name, i), align_bytes=64)
                half = J // 2
                nc.vector.tensor_copy(picked[:, 0:half], rows[:].indirect(offsets[:, 0:half // 16]))
                nc.scalar.activation(picked[:, half:J], rows[:].indirect(offsets[:, half // 16:J // 16]), ACT.Copy)
                pairs = picked[:].bitcast(F32)
                for u in range(2):
                    nc.tensor.transpose(turned[:, i, u, :], pairs[:, u:J // 2:2], ident[:])
            grouped = keep.tile([P, count * J], BF16, name=name + "_grouped", align_bytes=64)
            nc.scalar.copy(out=grouped[:].bitcast(F32).rearrange("p (i t u) -> p i t u", i=count, u=2),
                           in_=turned[:].rearrange("p i u t -> p i t u"))
            codes = keep.tile([P, count * P], U32, name=name + "_codes", align_bytes=64)
            plane = keep.tile([P, count * P], U8, name=name + "_plane", align_bytes=64)
            nc.vector.quantize_mx(out=codes[:].bitcast(FP8X4), scales=plane[:], in_=grouped[:])
            return codes, plane

        banks = [[sums.tile([P, 2, count * P], F32, name="bank%d_%d" % (first, h)) for h in range(2)]
                 for first, count in SPANS]

        def add_listed(s, codes, plane, weight_tile, weight_plane, closes):
            for nt in range(N_TILES):
                nc.tensor.matmul_mx(
                    out=banks[s][nt // 2][:, nt % 2, :],
                    lhsT=weight_tile(nt), lhsT_scale=weight_plane[:, 0, nt * P:(nt + 1) * P],
                    rhs=codes.bitcast(FP8X4), rhs_scale=plane,
                    start=False, stop=closes and nt % 2 == 1)

        def add_x(s, codes, plane):
            add_listed(s, codes, plane, lambda nt: wo_codes[:, 2 * nt * P:2 * (nt + 1) * P].bitcast(FP4X4),
                       wo_plane[:], False)

        def add_z(s, codes, plane, closes):
            add_listed(s, codes, plane, lambda nt: vo_codes[:, 4 * nt * P:4 * (nt + 1) * P].bitcast(FP8X4),
                       vo_plane[VO_ROW:P], closes)

        def add_base(s, passes, wb_codes, xb_codes, closes):
            first, count = SPANS[s]
            t0, t1 = first * P, (first + count) * P
            for nt in range(N_TILES):
                for i, z in enumerate(passes):
                    nc.tensor.matmul_mx(
                        out=banks[s][nt // 2][:, nt % 2, :],
                        lhsT=wb_codes[:, i, 4 * nt * P:4 * (nt + 1) * P].bitcast(FP8X4),
                        lhsT_scale=wb_plane[:, z, nt * P:(nt + 1) * P],
                        rhs=xb_codes[:, i, 2 * t0:2 * t1].bitcast(FP4X4), rhs_scale=xb_plane[:, z, t0:t1],
                        start=z == 0 and nt % 2 == 0, stop=closes and z == PASSES - 1 and nt % 2 == 1)

        out_tiles = out.rearrange("(c p) t -> p c t", p=P)

        def store(s):
            first, count = SPANS[s]
            t0, t1 = first * P, (first + count) * P
            low = keep.tile([P, 2, t1 - t0], F32, name="low%d" % s)
            nc.vector.tensor_tensor(low[:], banks[s][0][:], bias[:, 0:2].unsqueeze(2).to_broadcast([P, 2, t1 - t0]),
                                    mybir.AluOpType.add)
            nc.sync.dma_start(out=out_tiles[:, 0:2, t0:t1], in_=low[:])
            high = keep.tile([P, 2, t1 - t0], F32, name="high%d" % s)
            for i in range(2):
                nc.scalar.activation(high[:, i, :], banks[s][1][:, i, :], ACT.Identity, bias=bias[:, 2 + i:3 + i])
            nc.sync.dma_start(out=out_tiles[:, 2:4, t0:t1], in_=high[:])

        bias_turned = turn.tile([P, 1, 2, P], F32, name="turned")
        nc.tensor.transpose(bias_turned[:, 0, 0, :], bias_rows[:], ident[:])
        nc.vector.tensor_copy(bias[:], bias_turned[:, 0, 0, 0:N_TILES])

        x_first = quantise_listed([(x_rows[0], x_list), (x_rows[1], x_list)], "xq0")
        for s in range(len(SPANS)):
            add_base(s, range(EARLY), wb_early, xb_early, False)
        add_x(0, x_first[0][:], x_first[1][:])
        codes, plane = quantise_listed([(z_rows[0], z_list), (z_rows[1], z_list)], "zq0")
        add_z(0, codes[:], plane[:], False)
        codes, plane = quantise_listed([(x_rows[2], x_list), (z_rows[2], z_list)], "xz1")
        add_x(1, codes[:, 0:P], plane[:, 0:P])
        add_z(1, codes[:, P:2 * P], plane[:, P:2 * P], False)
        codes, plane = quantise_listed([(x_rows[3], x_list)], "xq2")
        for s in range(len(SPANS)):
            add_base(s, range(EARLY, PASSES), wb_late, xb_late, s < 2)
            if s < 2:
                store(s)
        add_x(2, codes[:], plane[:])
        codes, plane = quantise_listed([(z_rows[3], z_list)], "zq2")
        add_z(2, codes[:], plane[:], True)
        store(2)
